import numpy as np
import ml_dtypes


def mxq(x, axis, fmt="e4m3"):
    dtype, down = {"e4m3": (ml_dtypes.float8_e4m3fn, 7), "e5m2": (ml_dtypes.float8_e5m2, 14)}[fmt]
    v = np.moveaxis(np.asarray(x, np.float32).astype(ml_dtypes.bfloat16).astype(np.float64), axis, -1)
    blocks = v.reshape(v.shape[:-1] + (-1, 32))
    amax = np.abs(blocks).max(-1, keepdims=True)
    byte = np.maximum(np.where(amax > 0, np.frexp(amax)[1] - 1 + 127, 0) - down, 1)
    scale = np.exp2(byte - 127.0)
    codes = (blocks / scale).astype(np.float32).astype(dtype).astype(np.float64)
    return np.moveaxis((codes * scale).reshape(v.shape), -1, axis)


WIDE = False


def mx_kscale(k):
    if not WIDE:
        return np.ones(k)
    levels = np.array([10, -10, 5, -5, 0])
    if k % 512:
        return np.exp2(np.random.permutation(np.resize(levels, k // 32))).repeat(32)
    a = np.empty((k // 512, 16))
    for p in range(k // 512):
        a[p, :8] = np.random.permutation(np.resize(levels, 8))
        for g in range(8):
            far = levels[np.abs(levels - a[p, g]) >= 10]
            a[p, g + 8] = far[np.random.randint(len(far))]
    return np.exp2(a.ravel()).repeat(32)


def f64(x):
    return np.asarray(x).astype(np.float64)


def striped(idx):
    return np.tile(idx.reshape(-1, 16).T, (8, 1)).astype(np.uint16)


def unstriped(offs):
    return offs[:16].T.reshape(-1).astype(np.int64)


def striped8(idx):
    return np.concatenate([x.reshape(-1, 16).T for x in idx]).astype(np.uint16)


def runs(offs, k):
    lists = np.stack([offs[16 * r : 16 * r + 16].T.reshape(-1) for r in range(8)]).astype(np.int64)
    return lists[np.arange(k) % 512 // 64]


def pack_weight(w):
    k, n = w.shape
    w = f64(np.asarray(w, np.float32).astype(ml_dtypes.bfloat16)).reshape(k // 32, 32, n)
    amax = np.abs(w).max(1)
    byte = np.clip(np.where(amax > 0, np.frexp(amax)[1] - 1 + 127 - 7, 1), 1, 254)
    scaled = (w * np.exp2(127.0 - byte)[:, None, :]).reshape(k, n).astype(np.float32)
    words = np.ascontiguousarray(scaled.reshape(k // 512, 128, 4, n).transpose(0, 1, 3, 2)).astype(ml_dtypes.float8_e4m3fn).view(np.uint8)
    return words, np.ascontiguousarray(byte.astype(np.uint8).reshape(k // 512, 16, n))


def unpack_weight(words, scales):
    g, p, n, _ = words.shape
    vals = np.ascontiguousarray(words).view(ml_dtypes.float8_e4m3fn).astype(np.float64) * np.repeat(np.exp2(scales.astype(np.float64) - 127.0), 8, axis=1)[..., None]
    return vals.transpose(0, 1, 3, 2).reshape(g * 512, n)


def relu(v):
    return np.maximum(v, 0.0)


K, T, S, N, H, U = 512, 2048, 512, 512, 512, 1024


def setup_inputs():
    n = np.random.standard_normal
    s = mx_kscale(K)[:, None]
    u = mx_kscale(S)
    packed_xT = pack_weight(n((K, T)) * s)
    return {
        "x_words": packed_xT[0],
        "x_scales": packed_xT[1],
        "wa": (n((K, H)) / np.sqrt(K) / s).astype(np.float32),
        "wb": (n((K, H)) / np.sqrt(K) / s).astype(np.float32),
        "gt": (np.random.uniform(0.5, 1.5, (S, 1)) * u[:, None]).astype(np.float32),
        "w1": (n((S, N)) / np.sqrt(S) / u[:, None]).astype(np.float32),
        "offs": striped(np.random.permutation(T)[:S]),
        "two": striped(np.random.permutation(T)[:S]),
        "n1": striped8(np.stack([np.random.permutation(H) for _ in range(8)])),
        "n2": striped8(np.stack([np.random.permutation(H) for _ in range(8)])),
        "n3": striped8(np.stack([np.random.permutation(U)[:H] for _ in range(8)])),
        "n4": striped8(np.stack([np.random.permutation(H) for _ in range(8)])),
    }


def reference(x_words, x_scales, wa, wb, gt, w1, offs, two, n1, n2, n3, n4):
    xq = unpack_weight(x_words, x_scales)[:, unstriped(offs)]
    y = xq.T @ mxq(f64(wa), 0, "e4m3")
    x_two = unpack_weight(x_words, x_scales)[:, unstriped(two)]
    d = x_two.T @ mxq(f64(wb), 0, "e4m3")
    z = f64(gt) * (y * (np.tanh(d[np.arange(S)[:, None], runs(n1, S)] - (d[np.arange(S)[:, None], runs(n2, S)]))))
    h = mxq(f64(w1), 0, "e4m3").T @ mxq(z, 0, "e4m3")
    nw = h - (relu(h[np.arange(N)[:, None], runs(n4, N)]))
    out = np.zeros((N, U))
    out[np.arange(N)[:, None], runs(n3, N)] = nw
    return out

@@ -1,0 +1,192 @@
+from contextlib import ExitStack
+
+import concourse.mybir as mybir
+
+F32 = mybir.dt.float32
+BF16 = mybir.dt.bfloat16
+I32 = mybir.dt.int32
+U32 = mybir.dt.uint32
+U16 = mybir.dt.uint16
+U8 = mybir.dt.uint8
+FP8X4 = mybir.dt.float8_e4m3fn_x4
+ALU = mybir.AluOpType
+ACT = mybir.ActivationFunctionType
+
+P = 128
+PACK = 4
+K, T, S, N, H, U = 512, 2048, 512, 512, 512, 1024
+HALF = H // 2
+WB_PIECES = ((0, 256), (256, 384), (384, 512))
+FLOPS = 2 * (2 * K * S * H + S * N * H)
+
+
+def tile_picked_twtjointbpagez_none_p_kernel(tc, x_words, x_scales, wa, wb, gt, w1, offs, two, n1, n2, n3, n4, out):
+    nc = tc.nc
+    with ExitStack() as ctx:
+        keep = ctx.enter_context(tc.tile_pool(name="keep", bufs=1))
+        psum = ctx.enter_context(tc.psum_pool(name="psum", bufs=1))
+
+        def tile(name, shape, dtype, tag=None):
+            return keep.tile(shape, dtype, name=name, tag=tag or name, align_bytes=64)
+
+        def load_list(name, src):
+            lst = tile(name, [P, H // 16], U16)
+            nc.sync.dma_start(lst[:], src)
+            return lst
+
+        def half_of(lst, c):
+            return lst[:, c * HALF // 16 : (c + 1) * HALF // 16]
+
+        def cols(c):
+            return slice(c * HALF, (c + 1) * HALF)
+
+        xs = tile("xs", [P, T], U8)
+        nc.vector.memset(xs[:, : T // 2].bitcast(I32), 0)
+        nc.gpsimd.memset(xs[:, T // 2 :].bitcast(I32), 0)
+        warm = tile("warm", [P, 2], F32)
+        nc.vector.memset(warm[:, 0:1], 0.0)
+        nc.scalar.activation(warm[:, 1:2], warm[:, 0:1], ACT.Tanh)
+
+        two_l = load_list("two_l", two)
+        offs_l = load_list("offs_l", offs)
+        n2_l = load_list("n2_l", n2)
+        for q in range(4):
+            nc.sync.dma_start(xs[32 * q : 32 * q + 4, :].bitcast(I32), x_scales[0, 4 * q : 4 * q + 4, :].bitcast(I32))
+        xw = tile("xw", [P, T], I32)
+        nc.sync.dma_start(xw[:], x_words[0].rearrange("p n r -> p (n r)").bitcast(I32))
+        wb_raw = []
+        for c, (a, b) in enumerate(WB_PIECES):
+            raw = tile("wb_raw%d" % c, [P, PACK, b - a], F32)
+            nc.sync.dma_start(raw[:], wb.rearrange("(p j) n -> p j n", j=PACK)[:, :, a:b])
+            wb_raw.append(raw)
+        n1_l = load_list("n1_l", n1)
+        wa_raw = tile("wa_raw", [P, PACK, H], F32)
+        nc.sync.dma_start(wa_raw[:], wa.rearrange("(p j) n -> p j n", j=PACK))
+        gt_sb = tile("gt_sb", [P, PACK], F32)
+        nc.sync.dma_start(gt_sb[:], gt.rearrange("(p t) o -> p (t o)", t=PACK))
+        w1_raw = tile("w1_raw", [P, PACK, N], F32)
+        nc.sync.dma_start(w1_raw[:], w1.rearrange("(p j) n -> p j n", j=PACK))
+        n4_l = load_list("n4_l", n4)
+        n3_l = load_list("n3_l", n3)
+
+        page = [tile("page%d" % t, [P, U], F32) for t in range(PACK)]
+        for t in range(PACK):
+            nc.vector.memset(page[t][:], 0.0)
+
+        def pick_scales(name, lst):
+            got = tile(name + "_got", [P, S], U8)
+            nc.vector.tensor_copy(got[:], xs[:].indirect(lst[:]))
+            dealt = tile(name + "_dealt", [P, S], U8)
+            nc.vector.tensor_copy(dealt[:].rearrange("p (t m) -> p t m", t=PACK), got[:].rearrange("p (m t) -> p t m", t=PACK))
+            return dealt
+
+        def pick_words(name, lst):
+            dealt = tile(name, [P, S], U32)
+            nc.vector.tensor_copy(dealt[:].rearrange("p (t m) -> p m t", t=PACK), xw[:].bitcast(U32).indirect(lst[:]))
+            return dealt
+
+        def interleave(dst, src):
+            nc.scalar.copy(dst.rearrange("p (c i j) -> p c j i", i=4, j=PACK), src.rearrange("p j (c i) -> p c j i", i=4))
+
+        def quantize(codes, scales, src):
+            nc.vector.quantize_mx(out=codes.bitcast(FP8X4), scales=scales, in_=src)
+
+        def product(acc, lhs, lhs_scales, t, rhs, rhs_scales):
+            m = slice(t * P, (t + 1) * P)
+            nc.tensor.matmul_mx(out=acc, lhsT=lhs[:, m].bitcast(FP8X4), lhsT_scale=lhs_scales[:, m], rhs=rhs.bitcast(FP8X4), rhs_scale=rhs_scales, start=True, stop=True)
+
+        two_s = pick_scales("two_s", two_l)
+        offs_s = pick_scales("offs_s", offs_l)
+        wb_codes = tile("wb_codes", [P, H], U32, tag="wb_then_wa")
+        wb_scales = tile("wb_scales", [P, H], U8)
+        two_w = pick_words("two_w", two_l)
+        for c, (a, b) in enumerate(WB_PIECES):
+            wb16 = tile("wb16_%d" % c, [P, PACK * (b - a)], BF16)
+            interleave(wb16[:], wb_raw[c][:])
+            quantize(wb_codes[:, a:b], wb_scales[:, a:b], wb16[:])
+        offs_w = pick_words("offs_w", offs_l)
+
+        d_sb = []
+        for t in range(PACK):
+            d_ps = psum.tile([P, H], F32, name="d_ps%d" % t, tag="bank%d" % t)
+            product(d_ps[:], two_w, two_s, t, wb_codes[:], wb_scales[:])
+            d_t = tile("d_sb%d" % t, [P, H], F32)
+            nc.scalar.copy(d_t[:], d_ps[:])
+            d_sb.append(d_t)
+
+        wa16 = tile("wa16", [P, PACK * H], BF16, tag="wb_then_wa")
+        interleave(wa16[:], wa_raw[:])
+        wa_codes = tile("wa_codes", [P, H], U32)
+        wa_scales = tile("wa_scales", [P, H], U8)
+
+        w116 = tile("w116", [P, PACK * N], BF16)
+        nc.scalar.copy(w116[:].rearrange("p (t m j) -> p m j t", t=PACK, j=PACK), w1_raw[:].rearrange("p j (m t) -> p m j t", t=PACK))
+        diff = tile("diff", [P, PACK, H], F32)
+        th = tile("th", [P, PACK, H], F32)
+        gy = tile("gy", [P, PACK, H], F32)
+
+        def differences(t):
+            sub = tile("sub%d" % t, [P, H], F32, tag={2: "wb_then_wa", 3: "wa_raw"}.get(t))
+            for c in range(2):
+                nc.vector.tensor_copy(sub[:, cols(c)], d_sb[t][:].indirect(half_of(n2_l, c)))
+            for c in range(2):
+                nc.vector.tensor_tensor(diff[:, t, cols(c)], d_sb[t][:].indirect(half_of(n1_l, c)), sub[:, cols(c)], ALU.subtract)
+
+        def tanh_of(t):
+            for c in range(2):
+                nc.scalar.activation(th[:, t, cols(c)], diff[:, t, cols(c)], ACT.Tanh)
+
+        differences(0)
+        differences(1)
+        quantize(wa_codes[:], wa_scales[:], wa16[:])
+        tanh_of(0)
+        for t in range(PACK):
+            y_ps = psum.tile([P, H], F32, name="y_ps%d" % t, tag="bank%d" % (PACK + t))
+            product(y_ps[:], offs_w, offs_s, t, wa_codes[:], wa_scales[:])
+            nc.scalar.activation(gy[:, t, :], y_ps[:], ACT.Copy, scale=gt_sb[:, t : t + 1])
+        tanh_of(1)
+        differences(2)
+        tanh_of(2)
+        differences(3)
+        tanh_of(3)
+        w1_codes = tile("w1_codes", [P, N], U32, tag="wa_raw")
+        w1_scales = tile("w1_scales", [P, N], U8)
+        quantize(w1_codes[:], w1_scales[:], w116[:])
+
+        z_codes = tile("z_codes", [P, H], U32)
+        z_scales = tile("z_scales", [P, H], U8)
+        z16 = [tile("z16_%d" % c, [P, PACK * HALF], BF16) for c in range(2)]
+        for c in range(2):
+            nc.vector.tensor_tensor(
+                z16[c][:].rearrange("p (c i t) -> p c t i", i=4, t=PACK),
+                th[:, :, cols(c)].rearrange("p t (c i) -> p c t i", i=4),
+                gy[:, :, cols(c)].rearrange("p t (c i) -> p c t i", i=4),
+                ALU.mult,
+            )
+        h_ps = [psum.tile([P, H], F32, name="h_ps%d" % t, tag="bank%d" % t) for t in range(PACK)]
+        h_sb = [tile("h_sb%d" % t, [P, H], F32) for t in range(PACK)]
+        pos = [tile("pos%d" % t, [P, H], F32) for t in range(PACK)]
+        neg = [tile("neg%d" % t, [P, H], F32) for t in range(PACK)]
+        for c in range(2):
+            quantize(z_codes[:, cols(c)], z_scales[:, cols(c)], z16[c][:])
+            for t in range(PACK):
+                product(h_ps[t][:, cols(c)], w1_codes, w1_scales, t, z_codes[:, cols(c)], z_scales[:, cols(c)])
+                if t == 0:
+                    nc.scalar.activation(pos[t][:, cols(c)], h_ps[t][:, cols(c)], ACT.Relu)
+
+        def fetch(t):
+            if t > 0:
+                nc.scalar.activation(pos[t][:], h_ps[t][:], ACT.Relu)
+            for c in range(2):
+                nc.vector.tensor_scalar(neg[t][:, cols(c)], pos[t][:].indirect(half_of(n4_l, c)), -1.0, 0.0, ALU.mult, ALU.add)
+
+        def put(t):
+            nc.scalar.copy(h_sb[t][:], h_ps[t][:])
+            nc.vector.tensor_tensor(page[t][:].indirect(n3_l[:]), h_sb[t][:], neg[t][:], ALU.add)
+            nc.sync.dma_start(out.rearrange("(p t) u -> p t u", t=PACK)[:, t, :], page[t][:])
+
+        fetch(0)
+        for t in range(PACK):
+            if t + 1 < PACK:
+                fetch(t + 1)
+            put(t)

@@ -69,9 +69,14 @@ def tile_picked_twtjointbpagez_none_p_kernel(tc, x_words, x_scales, wa, wb, gt, 
         n4_l = load_list("n4_l", n4)
         n3_l = load_list("n3_l", n3)
 
-        page = [tile("page%d" % t, [P, U], F32) for t in range(PACK)]
-        for t in range(PACK):
+        page = {}
+
+        def clear_page(t, tag=None):
+            page[t] = tile("page%d" % t, [P, U], F32, tag=tag)
             nc.vector.memset(page[t][:], 0.0)
+
+        for t in range(PACK - 1):
+            clear_page(t)
 
         def pick_scales(name, lst):
             got = tile(name + "_got", [P, S], U8)
@@ -106,21 +111,19 @@ def tile_picked_twtjointbpagez_none_p_kernel(tc, x_words, x_scales, wa, wb, gt, 
             quantize(wb_codes[:, a:b], wb_scales[:, a:b], wb16[:])
         offs_w = pick_words("offs_w", offs_l)
 
-        d_sb = []
+        d_ps = [psum.tile([P, H], F32, name="d_ps%d" % t, tag="bank%d" % t) for t in range(PACK)]
+        d_sb = [tile("d_sb%d" % t, [P, H], F32) for t in range(PACK)]
         for t in range(PACK):
-            d_ps = psum.tile([P, H], F32, name="d_ps%d" % t, tag="bank%d" % t)
-            product(d_ps[:], two_w, two_s, t, wb_codes[:], wb_scales[:])
-            d_t = tile("d_sb%d" % t, [P, H], F32)
-            nc.scalar.copy(d_t[:], d_ps[:])
-            d_sb.append(d_t)
-
+            product(d_ps[t][:], two_w, two_s, t, wb_codes[:], wb_scales[:])
+        for t in range(2):
+            nc.scalar.copy(d_sb[t][:], d_ps[t][:])
         wa16 = tile("wa16", [P, PACK * H], BF16, tag="wb_then_wa")
         interleave(wa16[:], wa_raw[:])
+        for t in range(2, PACK):
+            nc.scalar.copy(d_sb[t][:], d_ps[t][:])
         wa_codes = tile("wa_codes", [P, H], U32)
         wa_scales = tile("wa_scales", [P, H], U8)
 
-        w116 = tile("w116", [P, PACK * N], BF16)
-        nc.scalar.copy(w116[:].rearrange("p (t m j) -> p m j t", t=PACK, j=PACK), w1_raw[:].rearrange("p j (m t) -> p m j t", t=PACK))
         diff = tile("diff", [P, PACK, H], F32)
         th = tile("th", [P, PACK, H], F32)
         gy = tile("gy", [P, PACK, H], F32)
@@ -133,8 +136,11 @@ def tile_picked_twtjointbpagez_none_p_kernel(tc, x_words, x_scales, wa, wb, gt, 
                 nc.vector.tensor_tensor(diff[:, t, cols(c)], d_sb[t][:].indirect(half_of(n1_l, c)), sub[:, cols(c)], ALU.subtract)
 
         def tanh_of(t):
-            for c in range(2):
-                nc.scalar.activation(th[:, t, cols(c)], diff[:, t, cols(c)], ACT.Tanh)
+            if t + 1 < PACK:
+                nc.scalar.activation(th[:, t, :], diff[:, t, :], ACT.Tanh)
+            else:
+                for c in range(2):
+                    nc.scalar.activation(th[:, t, cols(c)], diff[:, t, cols(c)], ACT.Tanh)
 
         differences(0)
         differences(1)
@@ -149,9 +155,11 @@ def tile_picked_twtjointbpagez_none_p_kernel(tc, x_words, x_scales, wa, wb, gt, 
         tanh_of(2)
         differences(3)
         tanh_of(3)
-        w1_codes = tile("w1_codes", [P, N], U32, tag="wa_raw")
+        w116 = tile("w116", [P, 2, PACK * N // 2], BF16, tag="wa_raw")
+        for u in range(2):
+            nc.scalar.copy(w116[:, u, :].rearrange("p (e m j) -> p m j e", e=2, j=PACK), w1_raw[:].rearrange("p j (m u e) -> p u m j e", u=2, e=2)[:, u])
+        w1_codes = tile("w1_codes", [P, N], U32)
         w1_scales = tile("w1_scales", [P, N], U8)
-        quantize(w1_codes[:], w1_scales[:], w116[:])
 
         z_codes = tile("z_codes", [P, H], U32)
         z_scales = tile("z_scales", [P, H], U8)
@@ -164,25 +172,34 @@ def tile_picked_twtjointbpagez_none_p_kernel(tc, x_words, x_scales, wa, wb, gt, 
                 ALU.mult,
             )
         h_ps = [psum.tile([P, H], F32, name="h_ps%d" % t, tag="bank%d" % t) for t in range(PACK)]
-        h_sb = [tile("h_sb%d" % t, [P, H], F32) for t in range(PACK)]
-        pos = [tile("pos%d" % t, [P, H], F32) for t in range(PACK)]
+        pos0 = tile("pos0", [P, H], F32)
+        h0 = tile("h0", [P, H], F32)
+        both = [None] + [tile("both%d" % t, [P, 2 * H], F32) for t in range(1, PACK)]
         neg = [tile("neg%d" % t, [P, H], F32) for t in range(PACK)]
+        quantize(w1_codes[:, cols(0)], w1_scales[:, cols(0)], w116[:, 0, :])
         for c in range(2):
             quantize(z_codes[:, cols(c)], z_scales[:, cols(c)], z16[c][:])
-            for t in range(PACK):
-                product(h_ps[t][:, cols(c)], w1_codes, w1_scales, t, z_codes[:, cols(c)], z_scales[:, cols(c)])
-                if t == 0:
-                    nc.scalar.activation(pos[t][:, cols(c)], h_ps[t][:, cols(c)], ACT.Relu)
+            product(h_ps[0][:, cols(c)], w1_codes, w1_scales, 0, z_codes[:, cols(c)], z_scales[:, cols(c)])
+            nc.scalar.activation(pos0[:, cols(c)], h_ps[0][:, cols(c)], ACT.Relu)
+        quantize(w1_codes[:, cols(1)], w1_scales[:, cols(1)], w116[:, 1, :])
+        for t in range(1, PACK):
+            product(h_ps[t][:], w1_codes, w1_scales, t, z_codes[:], z_scales[:])
+        clear_page(PACK - 1, tag="z16_1")
 
         def fetch(t):
-            if t > 0:
-                nc.scalar.activation(pos[t][:], h_ps[t][:], ACT.Relu)
-            for c in range(2):
-                nc.vector.tensor_scalar(neg[t][:, cols(c)], pos[t][:].indirect(half_of(n4_l, c)), -1.0, 0.0, ALU.mult, ALU.add)
+            if t == 0:
+                for c in range(2):
+                    nc.vector.tensor_scalar(neg[t][:, cols(c)], pos0[:].indirect(half_of(n4_l, c)), -1.0, 0.0, ALU.mult, ALU.add)
+            else:
+                nc.scalar.activation(both[t][:, :H], h_ps[t][:], ACT.Relu)
+                nc.scalar.copy(both[t][:, H:], h_ps[t][:])
+                nc.vector.tensor_scalar(neg[t][:], both[t][:].indirect(n4_l[:]), -1.0, 0.0, ALU.mult, ALU.add)
 
         def put(t):
-            nc.scalar.copy(h_sb[t][:], h_ps[t][:])
-            nc.vector.tensor_tensor(page[t][:].indirect(n3_l[:]), h_sb[t][:], neg[t][:], ALU.add)
+            if t == 0:
+                nc.scalar.copy(h0[:], h_ps[t][:])
+            h_t = h0[:] if t == 0 else both[t][:, H:]
+            nc.vector.tensor_tensor(page[t][:].indirect(n3_l[:]), h_t, neg[t][:], ALU.add)
             nc.sync.dma_start(out.rearrange("(p t) u -> p t u", t=PACK)[:, t, :], page[t][:])
 
         fetch(0)

@@ -71,12 +71,12 @@ def tile_picked_twtjointbpagez_none_p_kernel(tc, x_words, x_scales, wa, wb, gt, 
 
         page = {}
 
-        def clear_page(t, tag=None):
+        def clear_page(t, engine, tag=None):
             page[t] = tile("page%d" % t, [P, U], F32, tag=tag)
-            nc.vector.memset(page[t][:], 0.0)
+            engine.memset(page[t][:], 0.0)
 
         for t in range(PACK - 1):
-            clear_page(t)
+            clear_page(t, nc.vector)
 
         def pick_scales(name, lst):
             got = tile(name + "_got", [P, S], U8)
@@ -85,8 +85,8 @@ def tile_picked_twtjointbpagez_none_p_kernel(tc, x_words, x_scales, wa, wb, gt, 
             nc.vector.tensor_copy(dealt[:].rearrange("p (t m) -> p t m", t=PACK), got[:].rearrange("p (m t) -> p t m", t=PACK))
             return dealt
 
-        def pick_words(name, lst):
-            dealt = tile(name, [P, S], U32)
+        def pick_words(name, lst, tag=None):
+            dealt = tile(name, [P, S], U32, tag=tag)
             nc.vector.tensor_copy(dealt[:].rearrange("p (t m) -> p m t", t=PACK), xw[:].bitcast(U32).indirect(lst[:]))
             return dealt
 
@@ -109,7 +109,7 @@ def tile_picked_twtjointbpagez_none_p_kernel(tc, x_words, x_scales, wa, wb, gt, 
             wb16 = tile("wb16_%d" % c, [P, PACK * (b - a)], BF16)
             interleave(wb16[:], wb_raw[c][:])
             quantize(wb_codes[:, a:b], wb_scales[:, a:b], wb16[:])
-        offs_w = pick_words("offs_w", offs_l)
+        offs_w = pick_words("offs_w", offs_l, tag="wb_raw2")
 
         d_ps = [psum.tile([P, H], F32, name="d_ps%d" % t, tag="bank%d" % t) for t in range(PACK)]
         d_sb = [tile("d_sb%d" % t, [P, H], F32) for t in range(PACK)]
@@ -146,11 +146,11 @@ def tile_picked_twtjointbpagez_none_p_kernel(tc, x_words, x_scales, wa, wb, gt, 
         differences(1)
         quantize(wa_codes[:], wa_scales[:], wa16[:])
         tanh_of(0)
+        tanh_of(1)
         for t in range(PACK):
             y_ps = psum.tile([P, H], F32, name="y_ps%d" % t, tag="bank%d" % (PACK + t))
             product(y_ps[:], offs_w, offs_s, t, wa_codes[:], wa_scales[:])
             nc.scalar.activation(gy[:, t, :], y_ps[:], ACT.Copy, scale=gt_sb[:, t : t + 1])
-        tanh_of(1)
         differences(2)
         tanh_of(2)
         differences(3)
@@ -171,7 +171,8 @@ def tile_picked_twtjointbpagez_none_p_kernel(tc, x_words, x_scales, wa, wb, gt, 
                 gy[:, :, cols(c)].rearrange("p t (c i) -> p c t i", i=4),
                 ALU.mult,
             )
-        h_ps = [psum.tile([P, H], F32, name="h_ps%d" % t, tag="bank%d" % t) for t in range(PACK)]
+        h_ps = [None] + [psum.tile([P, H], F32, name="h_ps%d" % t, tag="bank%d" % t) for t in range(1, PACK)]
+        h0_ps = [psum.tile([P, HALF], F32, name="h0_ps%d" % c, tag="bank%d" % (PACK * c)) for c in range(2)]
         pos0 = tile("pos0", [P, H], F32)
         h0 = tile("h0", [P, H], F32)
         both = [None] + [tile("both%d" % t, [P, 2 * H], F32) for t in range(1, PACK)]
@@ -179,12 +180,12 @@ def tile_picked_twtjointbpagez_none_p_kernel(tc, x_words, x_scales, wa, wb, gt, 
         quantize(w1_codes[:, cols(0)], w1_scales[:, cols(0)], w116[:, 0, :])
         for c in range(2):
             quantize(z_codes[:, cols(c)], z_scales[:, cols(c)], z16[c][:])
-            product(h_ps[0][:, cols(c)], w1_codes, w1_scales, 0, z_codes[:, cols(c)], z_scales[:, cols(c)])
-            nc.scalar.activation(pos0[:, cols(c)], h_ps[0][:, cols(c)], ACT.Relu)
+            product(h0_ps[c][:], w1_codes, w1_scales, 0, z_codes[:, cols(c)], z_scales[:, cols(c)])
+            nc.scalar.activation(pos0[:, cols(c)], h0_ps[c][:], ACT.Relu)
         quantize(w1_codes[:, cols(1)], w1_scales[:, cols(1)], w116[:, 1, :])
         for t in range(1, PACK):
             product(h_ps[t][:], w1_codes, w1_scales, t, z_codes[:], z_scales[:])
-        clear_page(PACK - 1, tag="z16_1")
+        clear_page(PACK - 1, nc.gpsimd, tag="wa_raw")
 
         def fetch(t):
             if t == 0:
@@ -197,7 +198,8 @@ def tile_picked_twtjointbpagez_none_p_kernel(tc, x_words, x_scales, wa, wb, gt, 
 
         def put(t):
             if t == 0:
-                nc.scalar.copy(h0[:], h_ps[t][:])
+                for c in range(2):
+                    nc.scalar.copy(h0[:, cols(c)], h0_ps[c][:])
             h_t = h0[:] if t == 0 else both[t][:, H:]
             nc.vector.tensor_tensor(page[t][:].indirect(n3_l[:]), h_t, neg[t][:], ALU.add)
             nc.sync.dma_start(out.rearrange("(p t) u -> p t u", t=PACK)[:, t, :], page[t][:])

from contextlib import ExitStack

import concourse.mybir as mybir

F32 = mybir.dt.float32
BF16 = mybir.dt.bfloat16
I32 = mybir.dt.int32
U32 = mybir.dt.uint32
U16 = mybir.dt.uint16
U8 = mybir.dt.uint8
FP8X4 = mybir.dt.float8_e4m3fn_x4
ALU = mybir.AluOpType
ACT = mybir.ActivationFunctionType

P = 128
PACK = 4
K, T, S, N, H, U = 512, 2048, 512, 512, 512, 1024
HALF = H // 2
WB_PIECES = ((0, 256), (256, 384), (384, 512))
FLOPS = 2 * (2 * K * S * H + S * N * H)


def tile_picked_twtjointbpagez_none_p_kernel(tc, x_words, x_scales, wa, wb, gt, w1, offs, two, n1, n2, n3, n4, out):
    nc = tc.nc
    with ExitStack() as ctx:
        keep = ctx.enter_context(tc.tile_pool(name="keep", bufs=1))
        psum = ctx.enter_context(tc.psum_pool(name="psum", bufs=1))

        def tile(name, shape, dtype, tag=None):
            return keep.tile(shape, dtype, name=name, tag=tag or name, align_bytes=64)

        def load_list(name, src):
            lst = tile(name, [P, H // 16], U16)
            nc.sync.dma_start(lst[:], src)
            return lst

        def half_of(lst, c):
            return lst[:, c * HALF // 16 : (c + 1) * HALF // 16]

        def cols(c):
            return slice(c * HALF, (c + 1) * HALF)

        xs = tile("xs", [P, T], U8)
        nc.vector.memset(xs[:, : T // 2].bitcast(I32), 0)
        nc.gpsimd.memset(xs[:, T // 2 :].bitcast(I32), 0)
        warm = tile("warm", [P, 2], F32)
        nc.vector.memset(warm[:, 0:1], 0.0)
        nc.scalar.activation(warm[:, 1:2], warm[:, 0:1], ACT.Tanh)

        two_l = load_list("two_l", two)
        offs_l = load_list("offs_l", offs)
        n2_l = load_list("n2_l", n2)
        for q in range(4):
            nc.sync.dma_start(xs[32 * q : 32 * q + 4, :].bitcast(I32), x_scales[0, 4 * q : 4 * q + 4, :].bitcast(I32))
        xw = tile("xw", [P, T], I32)
        nc.sync.dma_start(xw[:], x_words[0].rearrange("p n r -> p (n r)").bitcast(I32))
        wb_raw = []
        for c, (a, b) in enumerate(WB_PIECES):
            raw = tile("wb_raw%d" % c, [P, PACK, b - a], F32)
            nc.sync.dma_start(raw[:], wb.rearrange("(p j) n -> p j n", j=PACK)[:, :, a:b])
            wb_raw.append(raw)
        n1_l = load_list("n1_l", n1)
        wa_raw = tile("wa_raw", [P, PACK, H], F32)
        nc.sync.dma_start(wa_raw[:], wa.rearrange("(p j) n -> p j n", j=PACK))
        gt_sb = tile("gt_sb", [P, PACK], F32)
        nc.sync.dma_start(gt_sb[:], gt.rearrange("(p t) o -> p (t o)", t=PACK))
        w1_raw = tile("w1_raw", [P, PACK, N], F32)
        nc.sync.dma_start(w1_raw[:], w1.rearrange("(p j) n -> p j n", j=PACK))
        n4_l = load_list("n4_l", n4)
        n3_l = load_list("n3_l", n3)

        page = {}

        def clear_page(t, engine, tag=None):
            page[t] = tile("page%d" % t, [P, U], F32, tag=tag)
            engine.memset(page[t][:], 0.0)

        for t in range(PACK - 1):
            clear_page(t, nc.vector)

        def pick_scales(name, lst):
            got = tile(name + "_got", [P, S], U8)
            nc.vector.tensor_copy(got[:], xs[:].indirect(lst[:]))
            dealt = tile(name + "_dealt", [P, S], U8)
            nc.vector.tensor_copy(dealt[:].rearrange("p (t m) -> p t m", t=PACK), got[:].rearrange("p (m t) -> p t m", t=PACK))
            return dealt

        def pick_words(name, lst, tag=None):
            dealt = tile(name, [P, S], U32, tag=tag)
            nc.vector.tensor_copy(dealt[:].rearrange("p (t m) -> p m t", t=PACK), xw[:].bitcast(U32).indirect(lst[:]))
            return dealt

        def interleave(dst, src):
            nc.scalar.copy(dst.rearrange("p (c i j) -> p c j i", i=4, j=PACK), src.rearrange("p j (c i) -> p c j i", i=4))

        def quantize(codes, scales, src):
            nc.vector.quantize_mx(out=codes.bitcast(FP8X4), scales=scales, in_=src)

        def product(acc, lhs, lhs_scales, t, rhs, rhs_scales):
            m = slice(t * P, (t + 1) * P)
            nc.tensor.matmul_mx(out=acc, lhsT=lhs[:, m].bitcast(FP8X4), lhsT_scale=lhs_scales[:, m], rhs=rhs.bitcast(FP8X4), rhs_scale=rhs_scales, start=True, stop=True)

        two_s = pick_scales("two_s", two_l)
        offs_s = pick_scales("offs_s", offs_l)
        wb_codes = tile("wb_codes", [P, H], U32, tag="wb_then_wa")
        wb_scales = tile("wb_scales", [P, H], U8)
        two_w = pick_words("two_w", two_l)
        for c, (a, b) in enumerate(WB_PIECES):
            wb16 = tile("wb16_%d" % c, [P, PACK * (b - a)], BF16)
            interleave(wb16[:], wb_raw[c][:])
            quantize(wb_codes[:, a:b], wb_scales[:, a:b], wb16[:])
        offs_w = pick_words("offs_w", offs_l, tag="wb_raw2")

        d_ps = [psum.tile([P, H], F32, name="d_ps%d" % t, tag="bank%d" % t) for t in range(PACK)]
        d_sb = [tile("d_sb%d" % t, [P, H], F32) for t in range(PACK)]
        for t in range(PACK):
            product(d_ps[t][:], two_w, two_s, t, wb_codes[:], wb_scales[:])
        for t in range(2):
            nc.scalar.copy(d_sb[t][:], d_ps[t][:])
        wa16 = tile("wa16", [P, PACK * H], BF16, tag="wb_then_wa")
        interleave(wa16[:], wa_raw[:])
        for t in range(2, PACK):
            nc.scalar.copy(d_sb[t][:], d_ps[t][:])
        wa_codes = tile("wa_codes", [P, H], U32)
        wa_scales = tile("wa_scales", [P, H], U8)

        diff = tile("diff", [P, PACK, H], F32)
        th = tile("th", [P, PACK, H], F32)
        gy = tile("gy", [P, PACK, H], F32)

        def differences(t):
            sub = tile("sub%d" % t, [P, H], F32, tag={2: "wb_then_wa", 3: "wa_raw"}.get(t))
            for c in range(2):
                nc.vector.tensor_copy(sub[:, cols(c)], d_sb[t][:].indirect(half_of(n2_l, c)))
            for c in range(2):
                nc.vector.tensor_tensor(diff[:, t, cols(c)], d_sb[t][:].indirect(half_of(n1_l, c)), sub[:, cols(c)], ALU.subtract)

        def tanh_of(t):
            if t + 1 < PACK:
                nc.scalar.activation(th[:, t, :], diff[:, t, :], ACT.Tanh)
            else:
                for c in range(2):
                    nc.scalar.activation(th[:, t, cols(c)], diff[:, t, cols(c)], ACT.Tanh)

        differences(0)
        differences(1)
        quantize(wa_codes[:], wa_scales[:], wa16[:])
        tanh_of(0)
        tanh_of(1)
        for t in range(PACK):
            y_ps = psum.tile([P, H], F32, name="y_ps%d" % t, tag="bank%d" % (PACK + t))
            product(y_ps[:], offs_w, offs_s, t, wa_codes[:], wa_scales[:])
            nc.scalar.activation(gy[:, t, :], y_ps[:], ACT.Copy, scale=gt_sb[:, t : t + 1])
        differences(2)
        tanh_of(2)
        differences(3)
        tanh_of(3)
        w116 = tile("w116", [P, 2, PACK * N // 2], BF16, tag="wa_raw")
        for u in range(2):
            nc.scalar.copy(w116[:, u, :].rearrange("p (e m j) -> p m j e", e=2, j=PACK), w1_raw[:].rearrange("p j (m u e) -> p u m j e", u=2, e=2)[:, u])
        w1_codes = tile("w1_codes", [P, N], U32)
        w1_scales = tile("w1_scales", [P, N], U8)

        z_codes = tile("z_codes", [P, H], U32)
        z_scales = tile("z_scales", [P, H], U8)
        z16 = [tile("z16_%d" % c, [P, PACK * HALF], BF16) for c in range(2)]
        for c in range(2):
            nc.vector.tensor_tensor(
                z16[c][:].rearrange("p (c i t) -> p c t i", i=4, t=PACK),
                th[:, :, cols(c)].rearrange("p t (c i) -> p c t i", i=4),
                gy[:, :, cols(c)].rearrange("p t (c i) -> p c t i", i=4),
                ALU.mult,
            )
        h_ps = [None] + [psum.tile([P, H], F32, name="h_ps%d" % t, tag="bank%d" % t) for t in range(1, PACK)]
        h0_ps = [psum.tile([P, HALF], F32, name="h0_ps%d" % c, tag="bank%d" % (PACK * c)) for c in range(2)]
        pos0 = tile("pos0", [P, H], F32)
        h0 = tile("h0", [P, H], F32)
        both = [None] + [tile("both%d" % t, [P, 2 * H], F32) for t in range(1, PACK)]
        neg = [tile("neg%d" % t, [P, H], F32) for t in range(PACK)]
        quantize(w1_codes[:, cols(0)], w1_scales[:, cols(0)], w116[:, 0, :])
        for c in range(2):
            quantize(z_codes[:, cols(c)], z_scales[:, cols(c)], z16[c][:])
            product(h0_ps[c][:], w1_codes, w1_scales, 0, z_codes[:, cols(c)], z_scales[:, cols(c)])
            nc.scalar.activation(pos0[:, cols(c)], h0_ps[c][:], ACT.Relu)
        quantize(w1_codes[:, cols(1)], w1_scales[:, cols(1)], w116[:, 1, :])
        for t in range(1, PACK):
            product(h_ps[t][:], w1_codes, w1_scales, t, z_codes[:], z_scales[:])
        clear_page(PACK - 1, nc.gpsimd, tag="wa_raw")

        def fetch(t):
            if t == 0:
                for c in range(2):
                    nc.vector.tensor_scalar(neg[t][:, cols(c)], pos0[:].indirect(half_of(n4_l, c)), -1.0, 0.0, ALU.mult, ALU.add)
            else:
                nc.scalar.activation(both[t][:, :H], h_ps[t][:], ACT.Relu)
                nc.scalar.copy(both[t][:, H:], h_ps[t][:])
                nc.vector.tensor_scalar(neg[t][:], both[t][:].indirect(n4_l[:]), -1.0, 0.0, ALU.mult, ALU.add)

        def put(t):
            if t == 0:
                for c in range(2):
                    nc.scalar.copy(h0[:, cols(c)], h0_ps[c][:])
            h_t = h0[:] if t == 0 else both[t][:, H:]
            nc.vector.tensor_tensor(page[t][:].indirect(n3_l[:]), h_t, neg[t][:], ALU.add)
            nc.sync.dma_start(out.rearrange("(p t) u -> p t u", t=PACK)[:, t, :], page[t][:])

        fetch(0)
        for t in range(PACK):
            if t + 1 < PACK:
                fetch(t + 1)
            put(t)
